import numpy as np
import ml_dtypes


def mxq(x, axis, fmt="e4m3"):
    dtype, down = {"e4m3": (ml_dtypes.float8_e4m3fn, 7), "e5m2": (ml_dtypes.float8_e5m2, 14)}[fmt]
    v = np.moveaxis(np.asarray(x, np.float32).astype(ml_dtypes.bfloat16).astype(np.float64), axis, -1)
    blocks = v.reshape(v.shape[:-1] + (-1, 32))
    amax = np.abs(blocks).max(-1, keepdims=True)
    byte = np.maximum(np.where(amax > 0, np.frexp(amax)[1] - 1 + 127, 0) - down, 1)
    scale = np.exp2(byte - 127.0)
    codes = (blocks / scale).astype(np.float32).astype(dtype).astype(np.float64)
    return np.moveaxis((codes * scale).reshape(v.shape), -1, axis)


WIDE = False


def mx_kscale(k):
    if not WIDE:
        return np.ones(k)
    levels = np.array([10, -10, 5, -5, 0])
    if k % 512:
        return np.exp2(np.random.permutation(np.resize(levels, k // 32))).repeat(32)
    a = np.empty((k // 512, 16))
    for p in range(k // 512):
        a[p, :8] = np.random.permutation(np.resize(levels, 8))
        for g in range(8):
            far = levels[np.abs(levels - a[p, g]) >= 10]
            a[p, g + 8] = far[np.random.randint(len(far))]
    return np.exp2(a.ravel()).repeat(32)


def f64(x):
    return np.asarray(x).astype(np.float64)


def striped(idx):
    return np.tile(idx.reshape(-1, 16).T, (8, 1)).astype(np.uint16)


def unstriped(offs):
    return offs[:16].T.reshape(-1).astype(np.int64)


E2M1 = np.array([0.0, 0.5, 1.0, 1.5, 2.0, 3.0, 4.0, 6.0, -0.0, -0.5, -1.0, -1.5, -2.0, -3.0, -4.0, -6.0])


def pack_weight(w, fmt):
    k, n = w.shape
    w = f64(np.asarray(w, np.float32).astype(ml_dtypes.bfloat16)).reshape(k // 32, 32, n)
    amax = np.abs(w).max(1)
    if fmt == "e4m3":
        byte = np.frexp(amax)[1] - 1 + 127 - 7
    else:
        mant, ex = np.frexp(amax / 6.0)
        byte = np.where(mant > 0.5, ex, ex - 1) + 127
    byte = np.clip(np.where(amax > 0, byte, 1), 1, 254)
    scaled = (w * np.exp2(127.0 - byte)[:, None, :]).reshape(k, n).astype(np.float32)
    by_word = np.ascontiguousarray(scaled.reshape(k // 512, 128, 4, n).transpose(0, 1, 3, 2))
    if fmt == "e4m3":
        words = by_word.astype(ml_dtypes.float8_e4m3fn).view(np.uint8)
    else:
        c = by_word.astype(ml_dtypes.float4_e2m1fn).view(np.uint8) & 0xF
        words = (c[..., 0::2] | (c[..., 1::2] << 4)).reshape(k // 512, 128, 2 * n)
    return np.ascontiguousarray(words), np.ascontiguousarray(byte.astype(np.uint8).reshape(k // 512, 16, n))


def unpack_weight(words, scales, fmt):
    g, _, n = scales.shape
    words = np.ascontiguousarray(words).reshape(g, 128, n, -1)
    if fmt == "e4m3":
        vals = words.view(ml_dtypes.float8_e4m3fn).astype(np.float64)
    else:
        nib = np.empty((g, 128, n, 4), np.uint8)
        nib[..., 0::2] = words & 0xF
        nib[..., 1::2] = words >> 4
        vals = E2M1[nib]
    vals = vals * np.repeat(np.exp2(scales.astype(np.float64) - 127.0), 8, axis=1)[..., None]
    return vals.transpose(0, 1, 3, 2).reshape(g * 512, n)


def sigmoid(v):
    return 1.0 / (1.0 + np.exp(-np.maximum(v, -700.0)))


K, T, E, C, H, N = 512, 2048, 8, 256, 512, 256


def by_expert(wq, xq):
    return np.concatenate([wq[e].T @ xq[:, e * C:(e + 1) * C] for e in range(E)], axis=1)


def setup_inputs():
    n = np.random.standard_normal
    s = mx_kscale(K)[:, None]
    u = mx_kscale(H)
    w1 = [pack_weight(m, "e2m1") for m in n((E, K, H)) / np.sqrt(K) / s[None]]
    w3 = [pack_weight(m, "e2m1") for m in n((E, K, H)) / np.sqrt(K) / s[None] * u[None, None, :]]
    w2 = [pack_weight(m, "e2m1") for m in n((E, H, N)) / np.sqrt(H) / u[None, :, None]]
    return {
        "xT": (n((K, T)) * s).astype(np.float32),
        "w1_words": np.stack([m[0] for m in w1]),
        "w1_scales": np.stack([m[1] for m in w1]),
        "w3_words": np.stack([m[0] for m in w3]),
        "w3_scales": np.stack([m[1] for m in w3]),
        "w2_words": np.stack([m[0] for m in w2]),
        "w2_scales": np.stack([m[1] for m in w2]),
        "gate": np.tile(np.random.uniform(0.2, 1.0, E * C), (N, 1)).astype(np.float32),
        "offs": striped(np.random.permutation(T)[:E * C]),
    }


def reference(xT, w1_words, w1_scales, w3_words, w3_scales, w2_words, w2_scales, gate, offs):
    idx = unstriped(offs)
    w1 = np.stack([unpack_weight(w1_words[e], w1_scales[e], "e2m1") for e in range(E)])
    w3 = np.stack([unpack_weight(w3_words[e], w3_scales[e], "e2m1") for e in range(E)])
    w2 = np.stack([unpack_weight(w2_words[e], w2_scales[e], "e2m1") for e in range(E)])
    xq = mxq(f64(xT)[:, idx], 0, "e4m3")
    h = sigmoid(by_expert(w1, xq))
    h = h * by_expert(w3, xq)
    y = by_expert(w2, mxq(h, 0, "e4m3"))
    out = np.zeros((N, T))
    out[:, idx] = f64(gate) * y
    return out

@@ -1,0 +1,206 @@
+from contextlib import ExitStack
+
+import concourse.mybir as mybir
+from concourse.masks import make_identity
+
+K, T, E, C, H, N = 512, 2048, 8, 256, 512, 256
+P = 128
+FLOPS = 2 * E * C * (2 * K * H + H * N)
+
+F32 = mybir.dt.float32
+BF16 = mybir.dt.bfloat16
+U32 = mybir.dt.uint32
+I32 = mybir.dt.int32
+U16 = mybir.dt.uint16
+U8 = mybir.dt.uint8
+FP8X4 = mybir.dt.float8_e4m3fn_x4
+FP4X4 = mybir.dt.float4_e2m1fn_x4
+MULT = mybir.AluOpType.mult
+SIGMOID = mybir.ActivationFunctionType.Sigmoid
+
+CHUNKS = [(0, 512), (512, 512), (1024, 512), (1536, 256), (1792, 256)]
+
+
+def tile_moe_pln_glu_sigmoid_kernel(
+    tc, xT, w1_words, w1_scales, w3_words, w3_scales, w2_words, w2_scales, gate, offs, out
+):
+    nc = tc.nc
+    with ExitStack() as ctx:
+        keep = ctx.enter_context(tc.tile_pool(name="keep", bufs=1))
+        ring = ctx.enter_context(tc.tile_pool(name="ring", bufs=3))
+        psum = ctx.enter_context(tc.psum_pool(name="psum", bufs=2))
+
+        offsets = keep.tile([P, E * C // 16], U16, name="offsets")
+        nc.sync.dma_start(offsets[:], offs)
+
+        warm = keep.tile([P, 1], F32, name="warm")
+        nc.vector.memset(warm[:], 0.0)
+        warm2 = keep.tile([P, 1], F32, name="warm2")
+        nc.scalar.activation(warm2[:], warm[:], SIGMOID)
+
+        bytes_all = keep.tile([P, T], U8, name="bytes_all", align_bytes=64)
+        nc.gpsimd.memset(bytes_all[:], 0)
+        s1 = keep.tile([P, E, H], U8, name="s1", align_bytes=64)
+        s3 = keep.tile([P, E, H], U8, name="s3", align_bytes=64)
+        s2 = keep.tile([P, E, N], U8, name="s2", align_bytes=64)
+        for s in (s1, s3, s2):
+            nc.gpsimd.memset(s[:].rearrange("p e i -> p (e i)").bitcast(I32), 0)
+        ident = keep.tile([P, P], F32, name="ident")
+        make_identity(nc, ident[:])
+
+        words_all = keep.tile([P, T], U32, name="words_all", align_bytes=64)
+        w1 = keep.tile([P, E, 2 * H], U8, name="w1", align_bytes=64)
+        w3 = keep.tile([P, E, 2 * H], U8, name="w3", align_bytes=64)
+        w2 = keep.tile([P, E, 2 * N], U8, name="w2", align_bytes=64)
+        gates = keep.tile([P, E * C], F32, name="gates")
+        windows = [keep.tile([P, T], F32, name=f"window{m}") for m in range(2)]
+
+        xrows = xT.rearrange("(p j) t -> p j t", j=4)
+        raws = []
+        for i, (c0, w) in enumerate(CHUNKS):
+            raw = keep.tile([P, 4, w], F32, name=f"raw{i}")
+            nc.sync.dma_start(raw[:], xrows[:, :, c0 : c0 + w])
+            raws.append(raw)
+
+        def load_scales(plane, dram):
+            for q in range(4):
+                nc.sync.dma_start(
+                    plane[32 * q : 32 * q + 4, :, :].bitcast(I32),
+                    dram[:, 0, 4 * q : 4 * q + 4, :].rearrange("e q i -> q e i").bitcast(I32),
+                )
+
+        def load_words(tile, dram, e0, e1):
+            nc.sync.dma_start(
+                tile[:, e0:e1, :].bitcast(I32),
+                dram[e0:e1, 0, :, :].rearrange("e p b -> p e b").bitcast(I32),
+            )
+
+        load_scales(s1, w1_scales)
+        load_words(w1, w1_words, 0, 1)
+        load_scales(s3, w3_scales)
+        load_words(w3, w3_words, 0, 1)
+        load_scales(s2, w2_scales)
+        load_words(w2, w2_words, 0, 2)
+        nc.sync.dma_start(gates[:, 0 : E * C // 2], gate[0:P, 0 : E * C // 2])
+        load_words(w1, w1_words, 1, 2)
+        load_words(w3, w3_words, 1, 2)
+        load_words(w1, w1_words, 2, 4)
+        load_words(w3, w3_words, 2, 4)
+        load_words(w2, w2_words, 2, 8)
+        load_words(w1, w1_words, 4, 8)
+        load_words(w3, w3_words, 4, 8)
+        nc.sync.dma_start(gates[:, E * C // 2 :], gate[0:P, E * C // 2 :])
+
+        for i, (c0, w) in enumerate(CHUNKS):
+            vec = w * 5 // 8
+            grouped = keep.tile([P, w, 4], BF16, name=f"grouped{i}", align_bytes=64)
+            turned = raws[i][:].rearrange("p j t -> p t j")
+            nc.scalar.copy(grouped[:, vec:w, :], turned[:, vec:w, :])
+            nc.vector.tensor_copy(grouped[:, 0:vec, :], turned[:, 0:vec, :])
+            nc.vector.quantize_mx(
+                out=words_all[:, c0 : c0 + w].bitcast(FP8X4),
+                scales=bytes_all[:, c0 : c0 + w],
+                in_=grouped[:].rearrange("p t j -> p (t j)"),
+            )
+
+        st = {}
+
+        def gather(e):
+            lst = offsets[:, 16 * e : 16 * e + 16]
+            gw = ring.tile([P, C], U32, name="gw", align_bytes=64)
+            gb = ring.tile([P, C], U8, name="gb", align_bytes=64)
+            nc.vector.tensor_copy(gw[:], words_all[:].indirect(lst))
+            nc.vector.tensor_copy(gb[:], bytes_all[:].indirect(lst))
+            st["g", e] = (gw, gb)
+
+        def first(e):
+            gw, gb = st["g", e]
+            for s in range(2):
+                cols = slice(128 * s, 128 * s + 128)
+                a = psum.tile([P, H], F32, name="a")
+                b = psum.tile([P, H], F32, name="b")
+                for o, w, sc in ((a, w1, s1), (b, w3, s3)):
+                    nc.tensor.matmul_mx(
+                        out=o[:],
+                        lhsT=gw[:, cols].bitcast(FP8X4),
+                        lhsT_scale=gb[:, cols],
+                        rhs=w[:, e, :].bitcast(FP4X4),
+                        rhs_scale=sc[:, e, :],
+                        start=True,
+                        stop=True,
+                    )
+                sig = ring.tile([P, H], F32, name="sig")
+                nc.scalar.activation(sig[:], a[:], SIGMOID)
+                st["ab", e, s] = (sig, b)
+
+        def hidden(e):
+            turned = psum.tile([P, 2 * C], F32, name="turned")
+            for s in range(2):
+                sig, b = st["ab", e, s]
+                h = ring.tile([P, H], BF16, name="h", align_bytes=64)
+                nc.vector.tensor_tensor(h[:], b[:], sig[:], MULT)
+                hw = h[:].bitcast(F32)
+                for u in range(2):
+                    nc.tensor.transpose(
+                        turned[:, C * u + 128 * s : C * u + 128 * s + 128],
+                        hw[:, u : H // 2 : 2],
+                        ident[:],
+                    )
+            hT = ring.tile([P, 4 * C], BF16, name="hT", align_bytes=64)
+            nc.scalar.copy(
+                hT[:].bitcast(F32).rearrange("p (n u) -> p n u", u=2),
+                turned[:].rearrange("p (u n) -> p n u", u=2),
+            )
+            st["h", e] = hT
+
+        def second(e):
+            hT = st["h", e]
+            hq = ring.tile([P, C], U32, name="hq", align_bytes=64)
+            hs = ring.tile([P, C], U8, name="hs", align_bytes=64)
+            nc.vector.quantize_mx(out=hq[:].bitcast(FP8X4), scales=hs[:], in_=hT[:])
+            y = psum.tile([P, 2, C], F32, name="y")
+            for m in range(2):
+                nc.tensor.matmul_mx(
+                    out=y[:, m, :],
+                    lhsT=w2[:, e, 256 * m : 256 * m + 256].bitcast(FP4X4),
+                    lhsT_scale=s2[:, e, 128 * m : 128 * m + 128],
+                    rhs=hq[:].bitcast(FP8X4),
+                    rhs_scale=hs[:],
+                    start=True,
+                    stop=True,
+                )
+            st["y", e] = y
+
+        def gated(e):
+            y = st["y", e]
+            yg = ring.tile([P, 2, C], F32, name="yg")
+            nc.vector.tensor_tensor(
+                yg[:],
+                y[:],
+                gates[:, C * e : C * e + C].unsqueeze(1).to_broadcast([P, 2, C]),
+                MULT,
+            )
+            st["yg", e] = yg
+
+        def scatter(e, m):
+            lst = offsets[:, 16 * e : 16 * e + 16]
+            nc.vector.tensor_copy(windows[m][:].indirect(lst), st["yg", e][:, m, :])
+
+        for i in range(E + 3):
+            if i < E:
+                gather(i)
+            if 0 <= i - 1 < E:
+                hidden(i - 1)
+            if i < E:
+                first(i)
+            if 0 <= i - 2 < E:
+                second(i - 2)
+            if 0 <= i - 3 < E:
+                gated(i - 3)
+                scatter(i - 3, 0)
+                if i - 3 < E - 2:
+                    scatter(i - 3, 1)
+        nc.sync.dma_start(out[0:P, :], windows[0][:])
+        scatter(E - 2, 1)
+        scatter(E - 1, 1)
+        nc.sync.dma_start(out[P : 2 * P, :], windows[1][:])

@@ -17,8 +17,11 @@ FP8X4 = mybir.dt.float8_e4m3fn_x4
 FP4X4 = mybir.dt.float4_e2m1fn_x4
 MULT = mybir.AluOpType.mult
 SIGMOID = mybir.ActivationFunctionType.Sigmoid
+COPY = mybir.ActivationFunctionType.Copy
 
-CHUNKS = [(0, 512), (512, 512), (1024, 512), (1536, 256), (1792, 256)]
+PAIR_CHUNKS = [(0, 1024), (1024, 512), (1536, 512)]
+PLANE_CHUNKS = {2: [(0, 1024), (1024, 1024)], 3: [(0, 1024), (1024, 512), (1536, 512)]}
+EARLY = 2
 
 
 def tile_moe_pln_glu_sigmoid_kernel(
@@ -27,7 +30,7 @@ def tile_moe_pln_glu_sigmoid_kernel(
     nc = tc.nc
     with ExitStack() as ctx:
         keep = ctx.enter_context(tc.tile_pool(name="keep", bufs=1))
-        ring = ctx.enter_context(tc.tile_pool(name="ring", bufs=3))
+        ring = ctx.enter_context(tc.tile_pool(name="ring", bufs=4))
         psum = ctx.enter_context(tc.psum_pool(name="psum", bufs=2))
 
         offsets = keep.tile([P, E * C // 16], U16, name="offsets")
@@ -38,17 +41,28 @@ def tile_moe_pln_glu_sigmoid_kernel(
         warm2 = keep.tile([P, 1], F32, name="warm2")
         nc.scalar.activation(warm2[:], warm[:], SIGMOID)
 
-        bytes_all = keep.tile([P, T], U8, name="bytes_all", align_bytes=64)
-        nc.gpsimd.memset(bytes_all[:], 0)
-        s1 = keep.tile([P, E, H], U8, name="s1", align_bytes=64)
-        s3 = keep.tile([P, E, H], U8, name="s3", align_bytes=64)
-        s2 = keep.tile([P, E, N], U8, name="s2", align_bytes=64)
-        for s in (s1, s3, s2):
-            nc.gpsimd.memset(s[:].rearrange("p e i -> p (e i)").bitcast(I32), 0)
+        def scale_plane(e_count, width, name):
+            plane = keep.tile([P, e_count, width], U8, name=name, align_bytes=64)
+            nc.gpsimd.memset(plane[:].rearrange("p e i -> p (e i)").bitcast(I32), 0)
+            return plane
+
+        def load_scales(queue, plane, dram, e0, e1):
+            for q in range(4):
+                queue.dma_start(
+                    plane[32 * q : 32 * q + 4, :, :].bitcast(I32),
+                    dram[e0:e1, 0, 4 * q : 4 * q + 4, :].rearrange("e q i -> q e i").bitcast(I32),
+                )
+
+        s1a = scale_plane(EARLY, H, "s1a")
+        load_scales(nc.gpsimd, s1a, w1_scales, 0, EARLY)
+        s3a = scale_plane(EARLY, H, "s3a")
+        load_scales(nc.gpsimd, s3a, w3_scales, 0, EARLY)
+        s1b = scale_plane(E - EARLY, H, "s1b")
+        s3b = scale_plane(E - EARLY, H, "s3b")
+        s2 = scale_plane(E, N, "s2")
         ident = keep.tile([P, P], F32, name="ident")
         make_identity(nc, ident[:])
 
-        words_all = keep.tile([P, T], U32, name="words_all", align_bytes=64)
         w1 = keep.tile([P, E, 2 * H], U8, name="w1", align_bytes=64)
         w3 = keep.tile([P, E, 2 * H], U8, name="w3", align_bytes=64)
         w2 = keep.tile([P, E, 2 * N], U8, name="w2", align_bytes=64)
@@ -56,18 +70,17 @@ def tile_moe_pln_glu_sigmoid_kernel(
         windows = [keep.tile([P, T], F32, name=f"window{m}") for m in range(2)]
 
         xrows = xT.rearrange("(p j) t -> p j t", j=4)
-        raws = []
-        for i, (c0, w) in enumerate(CHUNKS):
-            raw = keep.tile([P, 4, w], F32, name=f"raw{i}")
-            nc.sync.dma_start(raw[:], xrows[:, :, c0 : c0 + w])
-            raws.append(raw)
-
-        def load_scales(plane, dram):
-            for q in range(4):
-                nc.sync.dma_start(
-                    plane[32 * q : 32 * q + 4, :, :].bitcast(I32),
-                    dram[:, 0, 4 * q : 4 * q + 4, :].rearrange("e q i -> q e i").bitcast(I32),
-                )
+        raw_pair = []
+        for i, (c0, w) in enumerate(PAIR_CHUNKS):
+            raw = keep.tile([P, 2, w], F32, name=f"raw01_{i}")
+            nc.sync.dma_start(raw[:], xrows[:, 0:2, c0 : c0 + w])
+            raw_pair.append(raw)
+        raw_plane = {}
+        for j in (2, 3):
+            for c0, w in PLANE_CHUNKS[j]:
+                raw = keep.tile([P, w], F32, name=f"raw{j}_{c0}")
+                nc.sync.dma_start(raw[:], xrows[:, j, c0 : c0 + w])
+                raw_plane[j, c0] = raw
 
         def load_words(tile, dram, e0, e1):
             nc.sync.dma_start(
@@ -75,85 +88,119 @@ def tile_moe_pln_glu_sigmoid_kernel(
                 dram[e0:e1, 0, :, :].rearrange("e p b -> p e b").bitcast(I32),
             )
 
-        load_scales(s1, w1_scales)
+        half = E * C // 2
         load_words(w1, w1_words, 0, 1)
-        load_scales(s3, w3_scales)
         load_words(w3, w3_words, 0, 1)
-        load_scales(s2, w2_scales)
-        load_words(w2, w2_words, 0, 2)
-        nc.sync.dma_start(gates[:, 0 : E * C // 2], gate[0:P, 0 : E * C // 2])
         load_words(w1, w1_words, 1, 2)
         load_words(w3, w3_words, 1, 2)
+        load_scales(nc.sync, s2, w2_scales, 0, E)
+        load_words(w2, w2_words, 0, 2)
+        load_scales(nc.sync, s1b, w1_scales, EARLY, E)
+        load_scales(nc.sync, s3b, w3_scales, EARLY, E)
         load_words(w1, w1_words, 2, 4)
         load_words(w3, w3_words, 2, 4)
+        nc.sync.dma_start(gates[:, 0:half], gate[0:P, 0:half])
         load_words(w2, w2_words, 2, 8)
         load_words(w1, w1_words, 4, 8)
         load_words(w3, w3_words, 4, 8)
-        nc.sync.dma_start(gates[:, E * C // 2 :], gate[0:P, E * C // 2 :])
+        nc.sync.dma_start(gates[:, half:], gate[0:P, half:])
 
-        for i, (c0, w) in enumerate(CHUNKS):
-            vec = w * 5 // 8
-            grouped = keep.tile([P, w, 4], BF16, name=f"grouped{i}", align_bytes=64)
-            turned = raws[i][:].rearrange("p j t -> p t j")
-            nc.scalar.copy(grouped[:, vec:w, :], turned[:, vec:w, :])
-            nc.vector.tensor_copy(grouped[:, 0:vec, :], turned[:, 0:vec, :])
-            nc.vector.quantize_mx(
-                out=words_all[:, c0 : c0 + w].bitcast(FP8X4),
-                scales=bytes_all[:, c0 : c0 + w],
-                in_=grouped[:].rearrange("p t j -> p (t j)"),
-            )
+        pairs = keep.tile([P, T, 2], BF16, name="pairs", align_bytes=64)
+        for raw, (c0, w) in zip(raw_pair, PAIR_CHUNKS):
+            vec = w * 11 // 16
+            turned = raw[:].rearrange("p j t -> p t j")
+            nc.scalar.copy(pairs[:, c0 + vec : c0 + w, :], turned[:, vec:w, :])
+            nc.vector.tensor_copy(pairs[:, c0 : c0 + vec, :], turned[:, 0:vec, :])
+        pair_words = pairs[:].rearrange("p t j -> p (t j)").bitcast(U32)
+        planes = {}
+        for j in (2, 3):
+            plane = keep.tile([P, T], BF16, name=f"plane{j}", align_bytes=64)
+            for c0, w in PLANE_CHUNKS[j]:
+                nc.scalar.copy(plane[:, c0 : c0 + w], raw_plane[j, c0][:])
+            planes[j] = plane
 
         st = {}
 
-        def gather(e):
-            lst = offsets[:, 16 * e : 16 * e + 16]
-            gw = ring.tile([P, C], U32, name="gw", align_bytes=64)
-            gb = ring.tile([P, C], U8, name="gb", align_bytes=64)
-            nc.vector.tensor_copy(gw[:], words_all[:].indirect(lst))
-            nc.vector.tensor_copy(gb[:], bytes_all[:].indirect(lst))
-            st["g", e] = (gw, gb)
+        def offs_of(e):
+            return offsets[:, 16 * e : 16 * e + 16]
 
-        def first(e):
-            gw, gb = st["g", e]
-            for s in range(2):
-                cols = slice(128 * s, 128 * s + 128)
-                a = psum.tile([P, H], F32, name="a")
-                b = psum.tile([P, H], F32, name="b")
-                for o, w, sc in ((a, w1, s1), (b, w3, s3)):
-                    nc.tensor.matmul_mx(
-                        out=o[:],
-                        lhsT=gw[:, cols].bitcast(FP8X4),
-                        lhsT_scale=gb[:, cols],
-                        rhs=w[:, e, :].bitcast(FP4X4),
-                        rhs_scale=sc[:, e, :],
-                        start=True,
-                        stop=True,
-                    )
-                sig = ring.tile([P, H], F32, name="sig")
-                nc.scalar.activation(sig[:], a[:], SIGMOID)
-                st["ab", e, s] = (sig, b)
+        def gather_pair(e):
+            if not 0 <= e < E:
+                return
+            g = keep.tile([P, C, 4], BF16, name=f"g{e}", align_bytes=64)
+            words = g[:].rearrange("p n t -> p (n t)").bitcast(U32).rearrange("p (n u) -> p n u", u=2)
+            nc.vector.tensor_copy(words[:, :, 0], pair_words.indirect(offs_of(e)))
+            st["g", e] = g
 
-        def hidden(e):
-            turned = psum.tile([P, 2 * C], F32, name="turned")
-            for s in range(2):
-                sig, b = st["ab", e, s]
-                h = ring.tile([P, H], BF16, name="h", align_bytes=64)
-                nc.vector.tensor_tensor(h[:], b[:], sig[:], MULT)
-                hw = h[:].bitcast(F32)
-                for u in range(2):
-                    nc.tensor.transpose(
-                        turned[:, C * u + 128 * s : C * u + 128 * s + 128],
-                        hw[:, u : H // 2 : 2],
-                        ident[:],
-                    )
+        def gather_planes(e):
+            if not 0 <= e < E:
+                return
+            for j in (2, 3):
+                nc.scalar.activation(st["g", e][:, :, j], planes[j][:].indirect(offs_of(e)), COPY)
+
+        def quant1(e):
+            if not 0 <= e < E:
+                return
+            gq = ring.tile([P, C], U32, name="gq", align_bytes=64)
+            gs = ring.tile([P, C], U8, name="gs", align_bytes=64)
+            nc.vector.quantize_mx(
+                out=gq[:].bitcast(FP8X4), scales=gs[:], in_=st["g", e][:].rearrange("p n t -> p (n t)")
+            )
+            st["gq", e] = (gq, gs)
+
+        def first(e, s):
+            if not 0 <= e < E:
+                return
+            gq, gs = st["gq", e]
+            s1, s3, f = (s1a, s3a, e) if e < EARLY else (s1b, s3b, e - EARLY)
+            cols = slice(128 * s, 128 * s + 128)
+            a = psum.tile([P, H], F32, name="a")
+            b = psum.tile([P, H], F32, name="b")
+            for o, w, sc in ((a, w1, s1), (b, w3, s3)):
+                nc.tensor.matmul_mx(
+                    out=o[:],
+                    lhsT=gq[:, cols].bitcast(FP8X4),
+                    lhsT_scale=gs[:, cols],
+                    rhs=w[:, e, :].bitcast(FP4X4),
+                    rhs_scale=sc[:, f, :],
+                    start=True,
+                    stop=True,
+                )
+            sig = ring.tile([P, H], F32, name="sig")
+            nc.scalar.activation(sig[:], a[:], SIGMOID)
+            st["ab", e, s] = (sig, b)
+
+        def hidden(e, s):
+            if not 0 <= e < E:
+                return
+            if s == 0:
+                turned = psum.tile([P, 2 * C], F32, name="turned")
+                st["turned", e] = turned
+            turned = st["turned", e]
+            sig, b = st["ab", e, s]
+            h = ring.tile([P, H], BF16, name="h", align_bytes=64)
+            nc.vector.tensor_tensor(h[:], b[:], sig[:], MULT)
+            hw = h[:].bitcast(F32)
+            for u in range(2):
+                nc.tensor.transpose(
+                    turned[:, C * u + 128 * s : C * u + 128 * s + 128],
+                    hw[:, u : H // 2 : 2],
+                    ident[:],
+                )
+
+        def turn_out(e):
+            if not 0 <= e < E:
+                return
             hT = ring.tile([P, 4 * C], BF16, name="hT", align_bytes=64)
             nc.scalar.copy(
                 hT[:].bitcast(F32).rearrange("p (n u) -> p n u", u=2),
-                turned[:].rearrange("p (u n) -> p n u", u=2),
+                st["turned", e][:].rearrange("p (u n) -> p n u", u=2),
             )
             st["h", e] = hT
 
         def second(e):
+            if not 0 <= e < E:
+                return
             hT = st["h", e]
             hq = ring.tile([P, C], U32, name="hq", align_bytes=64)
             hs = ring.tile([P, C], U8, name="hs", align_bytes=64)
@@ -169,38 +216,43 @@ def tile_moe_pln_glu_sigmoid_kernel(
                     start=True,
                     stop=True,
                 )
-            st["y", e] = y
-
-        def gated(e):
-            y = st["y", e]
-            yg = ring.tile([P, 2, C], F32, name="yg")
-            nc.vector.tensor_tensor(
-                yg[:],
-                y[:],
-                gates[:, C * e : C * e + C].unsqueeze(1).to_broadcast([P, 2, C]),
-                MULT,
-            )
-            st["yg", e] = yg
+            ys = ring.tile([P, 2, C], F32, name="ys")
+            nc.scalar.copy(ys[:], y[:])
+            st["y", e] = ys
 
         def scatter(e, m):
-            lst = offsets[:, 16 * e : 16 * e + 16]
-            nc.vector.tensor_copy(windows[m][:].indirect(lst), st["yg", e][:, m, :])
+            if not 0 <= e < E:
+                return
+            nc.vector.tensor_tensor(
+                windows[m][:].indirect(offs_of(e)),
+                st["y", e][:, m, :],
+                gates[:, C * e : C * e + C],
+                MULT,
+            )
 
-        for i in range(E + 3):
-            if i < E:
-                gather(i)
-            if 0 <= i - 1 < E:
-                hidden(i - 1)
-            if i < E:
-                first(i)
-            if 0 <= i - 2 < E:
-                second(i - 2)
-            if 0 <= i - 3 < E:
-                gated(i - 3)
-                scatter(i - 3, 0)
-                if i - 3 < E - 2:
-                    scatter(i - 3, 1)
+        for e in range(4):
+            gather_pair(e)
+        gather_planes(0)
+        quant1(0)
+        first(0, 0)
+        first(0, 1)
+        gather_planes(1)
+        quant1(1)
+        gather_planes(2)
+        for i in range(1, E + 3):
+            gather_pair(i + 3)
+            hidden(i - 1, 0)
+            first(i, 0)
+            scatter(i - 3, 0)
+            hidden(i - 1, 1)
+            first(i, 1)
+            turn_out(i - 1)
+            quant1(i + 1)
+            gather_planes(i + 2)
+            if i - 3 < E - 3:
+                scatter(i - 3, 1)
+            second(i - 1)
         nc.sync.dma_start(out[0:P, :], windows[0][:])
-        scatter(E - 2, 1)
-        scatter(E - 1, 1)
+        for e in range(E - 3, E):
+            scatter(e, 1)
         nc.sync.dma_start(out[P : 2 * P, :], windows[1][:])

@@ -17,11 +17,9 @@ FP8X4 = mybir.dt.float8_e4m3fn_x4
 FP4X4 = mybir.dt.float4_e2m1fn_x4
 MULT = mybir.AluOpType.mult
 SIGMOID = mybir.ActivationFunctionType.Sigmoid
-COPY = mybir.ActivationFunctionType.Copy
 
-PAIR_CHUNKS = [(0, 1024), (1024, 512), (1536, 512)]
-PLANE_CHUNKS = {2: [(0, 1024), (1024, 1024)], 3: [(0, 1024), (1024, 512), (1536, 512)]}
-EARLY = 2
+CHUNKS = [(0, 1024), (1024, 512), (1536, 256), (1792, 256)]
+EARLY = 3
 
 
 def tile_moe_pln_glu_sigmoid_kernel(
@@ -34,7 +32,6 @@ def tile_moe_pln_glu_sigmoid_kernel(
         psum = ctx.enter_context(tc.psum_pool(name="psum", bufs=2))
 
         offsets = keep.tile([P, E * C // 16], U16, name="offsets")
-        nc.sync.dma_start(offsets[:], offs)
 
         warm = keep.tile([P, 1], F32, name="warm")
         nc.vector.memset(warm[:], 0.0)
@@ -53,6 +50,9 @@ def tile_moe_pln_glu_sigmoid_kernel(
                     dram[e0:e1, 0, 4 * q : 4 * q + 4, :].rearrange("e q i -> q e i").bitcast(I32),
                 )
 
+        bytes_all = keep.tile([P, T], U8, name="bytes_all", align_bytes=64)
+        words_all = keep.tile([P, T], U32, name="words_all", align_bytes=64)
+        nc.gpsimd.memset(bytes_all[:], 0)
         s1a = scale_plane(EARLY, H, "s1a")
         load_scales(nc.gpsimd, s1a, w1_scales, 0, EARLY)
         s3a = scale_plane(EARLY, H, "s3a")
@@ -70,17 +70,13 @@ def tile_moe_pln_glu_sigmoid_kernel(
         windows = [keep.tile([P, T], F32, name=f"window{m}") for m in range(2)]
 
         xrows = xT.rearrange("(p j) t -> p j t", j=4)
-        raw_pair = []
-        for i, (c0, w) in enumerate(PAIR_CHUNKS):
-            raw = keep.tile([P, 2, w], F32, name=f"raw01_{i}")
-            nc.sync.dma_start(raw[:], xrows[:, 0:2, c0 : c0 + w])
-            raw_pair.append(raw)
-        raw_plane = {}
-        for j in (2, 3):
-            for c0, w in PLANE_CHUNKS[j]:
-                raw = keep.tile([P, w], F32, name=f"raw{j}_{c0}")
-                nc.sync.dma_start(raw[:], xrows[:, j, c0 : c0 + w])
-                raw_plane[j, c0] = raw
+        raws = []
+        for i, (c0, w) in enumerate(CHUNKS):
+            raw = keep.tile([P, 4, w], F32, name=f"raw{i}")
+            nc.sync.dma_start(raw[:], xrows[:, :, c0 : c0 + w])
+            raws.append(raw)
+            if i == 0:
+                nc.sync.dma_start(offsets[:], offs)
 
         def load_words(tile, dram, e0, e1):
             nc.sync.dma_start(
@@ -88,64 +84,51 @@ def tile_moe_pln_glu_sigmoid_kernel(
                 dram[e0:e1, 0, :, :].rearrange("e p b -> p e b").bitcast(I32),
             )
 
-        half = E * C // 2
-        load_words(w1, w1_words, 0, 1)
-        load_words(w3, w3_words, 0, 1)
-        load_words(w1, w1_words, 1, 2)
-        load_words(w3, w3_words, 1, 2)
-        load_scales(nc.sync, s2, w2_scales, 0, E)
+        def load_gates(c0, c1):
+            nc.sync.dma_start(gates[:, c0:c1], gate[0:P, c0:c1])
+
+        for e in range(2):
+            load_words(w1, w1_words, e, e + 1)
+            load_words(w3, w3_words, e, e + 1)
         load_words(w2, w2_words, 0, 2)
+        load_words(w1, w1_words, 2, 3)
+        load_words(w3, w3_words, 2, 3)
+        load_scales(nc.sync, s2, w2_scales, 0, E)
         load_scales(nc.sync, s1b, w1_scales, EARLY, E)
         load_scales(nc.sync, s3b, w3_scales, EARLY, E)
-        load_words(w1, w1_words, 2, 4)
-        load_words(w3, w3_words, 2, 4)
-        nc.sync.dma_start(gates[:, 0:half], gate[0:P, 0:half])
+        load_gates(0, 512)
+        load_words(w1, w1_words, 3, 5)
+        load_words(w3, w3_words, 3, 5)
         load_words(w2, w2_words, 2, 8)
-        load_words(w1, w1_words, 4, 8)
-        load_words(w3, w3_words, 4, 8)
-        nc.sync.dma_start(gates[:, half:], gate[0:P, half:])
+        load_gates(512, 1280)
+        load_words(w1, w1_words, 5, 8)
+        load_words(w3, w3_words, 5, 8)
+        load_gates(1280, 2048)
 
-        pairs = keep.tile([P, T, 2], BF16, name="pairs", align_bytes=64)
-        for raw, (c0, w) in zip(raw_pair, PAIR_CHUNKS):
-            vec = w * 11 // 16
-            turned = raw[:].rearrange("p j t -> p t j")
-            nc.scalar.copy(pairs[:, c0 + vec : c0 + w, :], turned[:, vec:w, :])
-            nc.vector.tensor_copy(pairs[:, c0 : c0 + vec, :], turned[:, 0:vec, :])
-        pair_words = pairs[:].rearrange("p t j -> p (t j)").bitcast(U32)
-        planes = {}
-        for j in (2, 3):
-            plane = keep.tile([P, T], BF16, name=f"plane{j}", align_bytes=64)
-            for c0, w in PLANE_CHUNKS[j]:
-                nc.scalar.copy(plane[:, c0 : c0 + w], raw_plane[j, c0][:])
-            planes[j] = plane
+        for i, (c0, w) in enumerate(CHUNKS):
+            vec = w * 5 // 8
+            grouped = keep.tile([P, w, 4], BF16, name=f"grouped{i}", align_bytes=64)
+            turned = raws[i][:].rearrange("p j t -> p t j")
+            nc.scalar.copy(grouped[:, vec:w, :], turned[:, vec:w, :])
+            nc.vector.tensor_copy(grouped[:, 0:vec, :], turned[:, 0:vec, :])
+            nc.vector.quantize_mx(
+                out=words_all[:, c0 : c0 + w].bitcast(FP8X4),
+                scales=bytes_all[:, c0 : c0 + w],
+                in_=grouped[:].rearrange("p t j -> p (t j)"),
+            )
 
         st = {}
 
         def offs_of(e):
             return offsets[:, 16 * e : 16 * e + 16]
 
-        def gather_pair(e):
-            if not 0 <= e < E:
-                return
-            g = keep.tile([P, C, 4], BF16, name=f"g{e}", align_bytes=64)
-            words = g[:].rearrange("p n t -> p (n t)").bitcast(U32).rearrange("p (n u) -> p n u", u=2)
-            nc.vector.tensor_copy(words[:, :, 0], pair_words.indirect(offs_of(e)))
-            st["g", e] = g
-
-        def gather_planes(e):
-            if not 0 <= e < E:
-                return
-            for j in (2, 3):
-                nc.scalar.activation(st["g", e][:, :, j], planes[j][:].indirect(offs_of(e)), COPY)
-
-        def quant1(e):
+        def gather(e):
             if not 0 <= e < E:
                 return
             gq = ring.tile([P, C], U32, name="gq", align_bytes=64)
             gs = ring.tile([P, C], U8, name="gs", align_bytes=64)
-            nc.vector.quantize_mx(
-                out=gq[:].bitcast(FP8X4), scales=gs[:], in_=st["g", e][:].rearrange("p n t -> p (n t)")
-            )
+            nc.vector.tensor_copy(gq[:], words_all[:].indirect(offs_of(e)))
+            nc.vector.tensor_copy(gs[:], bytes_all[:].indirect(offs_of(e)))
             st["gq", e] = (gq, gs)
 
         def first(e, s):
@@ -179,12 +162,17 @@ def tile_moe_pln_glu_sigmoid_kernel(
             turned = st["turned", e]
             sig, b = st["ab", e, s]
             h = ring.tile([P, H], BF16, name="h", align_bytes=64)
-            nc.vector.tensor_tensor(h[:], b[:], sig[:], MULT)
+            nc.vector.tensor_tensor(
+                h[:].rearrange("p (u w d) -> p w u d", u=2, d=2),
+                b[:].rearrange("p (w u d) -> p w u d", u=2, d=2),
+                sig[:].rearrange("p (w u d) -> p w u d", u=2, d=2),
+                MULT,
+            )
             hw = h[:].bitcast(F32)
             for u in range(2):
                 nc.tensor.transpose(
                     turned[:, C * u + 128 * s : C * u + 128 * s + 128],
-                    hw[:, u : H // 2 : 2],
+                    hw[:, 128 * u : 128 * u + 128],
                     ident[:],
                 )
 
@@ -230,29 +218,24 @@ def tile_moe_pln_glu_sigmoid_kernel(
                 MULT,
             )
 
-        for e in range(4):
-            gather_pair(e)
-        gather_planes(0)
-        quant1(0)
+        gather(0)
         first(0, 0)
         first(0, 1)
-        gather_planes(1)
-        quant1(1)
-        gather_planes(2)
+        gather(1)
         for i in range(1, E + 3):
-            gather_pair(i + 3)
             hidden(i - 1, 0)
             first(i, 0)
             scatter(i - 3, 0)
             hidden(i - 1, 1)
             first(i, 1)
             turn_out(i - 1)
-            quant1(i + 1)
-            gather_planes(i + 2)
+            gather(i + 1)
             if i - 3 < E - 3:
                 scatter(i - 3, 1)
+            elif i - 3 == E - 2:
+                scatter(E - 3, 1)
             second(i - 1)
         nc.sync.dma_start(out[0:P, :], windows[0][:])
-        for e in range(E - 3, E):
+        for e in range(E - 2, E):
             scatter(e, 1)
         nc.sync.dma_start(out[P : 2 * P, :], windows[1][:])

@@ -18,7 +18,7 @@ FP4X4 = mybir.dt.float4_e2m1fn_x4
 MULT = mybir.AluOpType.mult
 SIGMOID = mybir.ActivationFunctionType.Sigmoid
 
-CHUNKS = [(0, 1024), (1024, 512), (1536, 256), (1792, 256)]
+CHUNKS = [(0, 512), (512, 512), (1024, 512), (1536, 256), (1792, 256)]
 EARLY = 3
 
 
@@ -40,7 +40,7 @@ def tile_moe_pln_glu_sigmoid_kernel(
 
         def scale_plane(e_count, width, name):
             plane = keep.tile([P, e_count, width], U8, name=name, align_bytes=64)
-            nc.gpsimd.memset(plane[:].rearrange("p e i -> p (e i)").bitcast(I32), 0)
+            nc.vector.memset(plane[:].rearrange("p e i -> p (e i)").bitcast(I32), 0)
             return plane
 
         def load_scales(queue, plane, dram, e0, e1):
@@ -53,15 +53,13 @@ def tile_moe_pln_glu_sigmoid_kernel(
         bytes_all = keep.tile([P, T], U8, name="bytes_all", align_bytes=64)
         words_all = keep.tile([P, T], U32, name="words_all", align_bytes=64)
         nc.gpsimd.memset(bytes_all[:], 0)
+        ident = keep.tile([P, P], F32, name="ident")
+        make_identity(nc, ident[:])
         s1a = scale_plane(EARLY, H, "s1a")
-        load_scales(nc.gpsimd, s1a, w1_scales, 0, EARLY)
         s3a = scale_plane(EARLY, H, "s3a")
-        load_scales(nc.gpsimd, s3a, w3_scales, 0, EARLY)
         s1b = scale_plane(E - EARLY, H, "s1b")
         s3b = scale_plane(E - EARLY, H, "s3b")
         s2 = scale_plane(E, N, "s2")
-        ident = keep.tile([P, P], F32, name="ident")
-        make_identity(nc, ident[:])
 
         w1 = keep.tile([P, E, 2 * H], U8, name="w1", align_bytes=64)
         w3 = keep.tile([P, E, 2 * H], U8, name="w3", align_bytes=64)
@@ -75,8 +73,12 @@ def tile_moe_pln_glu_sigmoid_kernel(
             raw = keep.tile([P, 4, w], F32, name=f"raw{i}")
             nc.sync.dma_start(raw[:], xrows[:, :, c0 : c0 + w])
             raws.append(raw)
-            if i == 0:
+            if i == 1:
                 nc.sync.dma_start(offsets[:], offs)
+            if i == 2:
+                load_scales(nc.sync, s1a, w1_scales, 0, EARLY)
+            if i == 4:
+                load_scales(nc.sync, s3a, w3_scales, 0, EARLY)
 
         def load_words(tile, dram, e0, e1):
             nc.sync.dma_start(

from contextlib import ExitStack

import concourse.mybir as mybir
from concourse.masks import make_identity

K, T, E, C, H, N = 512, 2048, 8, 256, 512, 256
P = 128
FLOPS = 2 * E * C * (2 * K * H + H * N)

F32 = mybir.dt.float32
BF16 = mybir.dt.bfloat16
U32 = mybir.dt.uint32
I32 = mybir.dt.int32
U16 = mybir.dt.uint16
U8 = mybir.dt.uint8
FP8X4 = mybir.dt.float8_e4m3fn_x4
FP4X4 = mybir.dt.float4_e2m1fn_x4
MULT = mybir.AluOpType.mult
SIGMOID = mybir.ActivationFunctionType.Sigmoid

CHUNKS = [(0, 512), (512, 512), (1024, 512), (1536, 256), (1792, 256)]
EARLY = 3


def tile_moe_pln_glu_sigmoid_kernel(
    tc, xT, w1_words, w1_scales, w3_words, w3_scales, w2_words, w2_scales, gate, offs, out
):
    nc = tc.nc
    with ExitStack() as ctx:
        keep = ctx.enter_context(tc.tile_pool(name="keep", bufs=1))
        ring = ctx.enter_context(tc.tile_pool(name="ring", bufs=4))
        psum = ctx.enter_context(tc.psum_pool(name="psum", bufs=2))

        offsets = keep.tile([P, E * C // 16], U16, name="offsets")

        warm = keep.tile([P, 1], F32, name="warm")
        nc.vector.memset(warm[:], 0.0)
        warm2 = keep.tile([P, 1], F32, name="warm2")
        nc.scalar.activation(warm2[:], warm[:], SIGMOID)

        def scale_plane(e_count, width, name):
            plane = keep.tile([P, e_count, width], U8, name=name, align_bytes=64)
            nc.vector.memset(plane[:].rearrange("p e i -> p (e i)").bitcast(I32), 0)
            return plane

        def load_scales(queue, plane, dram, e0, e1):
            for q in range(4):
                queue.dma_start(
                    plane[32 * q : 32 * q + 4, :, :].bitcast(I32),
                    dram[e0:e1, 0, 4 * q : 4 * q + 4, :].rearrange("e q i -> q e i").bitcast(I32),
                )

        bytes_all = keep.tile([P, T], U8, name="bytes_all", align_bytes=64)
        words_all = keep.tile([P, T], U32, name="words_all", align_bytes=64)
        nc.gpsimd.memset(bytes_all[:], 0)
        ident = keep.tile([P, P], F32, name="ident")
        make_identity(nc, ident[:])
        s1a = scale_plane(EARLY, H, "s1a")
        s3a = scale_plane(EARLY, H, "s3a")
        s1b = scale_plane(E - EARLY, H, "s1b")
        s3b = scale_plane(E - EARLY, H, "s3b")
        s2 = scale_plane(E, N, "s2")

        w1 = keep.tile([P, E, 2 * H], U8, name="w1", align_bytes=64)
        w3 = keep.tile([P, E, 2 * H], U8, name="w3", align_bytes=64)
        w2 = keep.tile([P, E, 2 * N], U8, name="w2", align_bytes=64)
        gates = keep.tile([P, E * C], F32, name="gates")
        windows = [keep.tile([P, T], F32, name=f"window{m}") for m in range(2)]

        xrows = xT.rearrange("(p j) t -> p j t", j=4)
        raws = []
        for i, (c0, w) in enumerate(CHUNKS):
            raw = keep.tile([P, 4, w], F32, name=f"raw{i}")
            nc.sync.dma_start(raw[:], xrows[:, :, c0 : c0 + w])
            raws.append(raw)
            if i == 1:
                nc.sync.dma_start(offsets[:], offs)
            if i == 2:
                load_scales(nc.sync, s1a, w1_scales, 0, EARLY)
            if i == 4:
                load_scales(nc.sync, s3a, w3_scales, 0, EARLY)

        def load_words(tile, dram, e0, e1):
            nc.sync.dma_start(
                tile[:, e0:e1, :].bitcast(I32),
                dram[e0:e1, 0, :, :].rearrange("e p b -> p e b").bitcast(I32),
            )

        def load_gates(c0, c1):
            nc.sync.dma_start(gates[:, c0:c1], gate[0:P, c0:c1])

        for e in range(2):
            load_words(w1, w1_words, e, e + 1)
            load_words(w3, w3_words, e, e + 1)
        load_words(w2, w2_words, 0, 2)
        load_words(w1, w1_words, 2, 3)
        load_words(w3, w3_words, 2, 3)
        load_scales(nc.sync, s2, w2_scales, 0, E)
        load_scales(nc.sync, s1b, w1_scales, EARLY, E)
        load_scales(nc.sync, s3b, w3_scales, EARLY, E)
        load_gates(0, 512)
        load_words(w1, w1_words, 3, 5)
        load_words(w3, w3_words, 3, 5)
        load_words(w2, w2_words, 2, 8)
        load_gates(512, 1280)
        load_words(w1, w1_words, 5, 8)
        load_words(w3, w3_words, 5, 8)
        load_gates(1280, 2048)

        for i, (c0, w) in enumerate(CHUNKS):
            vec = w * 5 // 8
            grouped = keep.tile([P, w, 4], BF16, name=f"grouped{i}", align_bytes=64)
            turned = raws[i][:].rearrange("p j t -> p t j")
            nc.scalar.copy(grouped[:, vec:w, :], turned[:, vec:w, :])
            nc.vector.tensor_copy(grouped[:, 0:vec, :], turned[:, 0:vec, :])
            nc.vector.quantize_mx(
                out=words_all[:, c0 : c0 + w].bitcast(FP8X4),
                scales=bytes_all[:, c0 : c0 + w],
                in_=grouped[:].rearrange("p t j -> p (t j)"),
            )

        st = {}

        def offs_of(e):
            return offsets[:, 16 * e : 16 * e + 16]

        def gather(e):
            if not 0 <= e < E:
                return
            gq = ring.tile([P, C], U32, name="gq", align_bytes=64)
            gs = ring.tile([P, C], U8, name="gs", align_bytes=64)
            nc.vector.tensor_copy(gq[:], words_all[:].indirect(offs_of(e)))
            nc.vector.tensor_copy(gs[:], bytes_all[:].indirect(offs_of(e)))
            st["gq", e] = (gq, gs)

        def first(e, s):
            if not 0 <= e < E:
                return
            gq, gs = st["gq", e]
            s1, s3, f = (s1a, s3a, e) if e < EARLY else (s1b, s3b, e - EARLY)
            cols = slice(128 * s, 128 * s + 128)
            a = psum.tile([P, H], F32, name="a")
            b = psum.tile([P, H], F32, name="b")
            for o, w, sc in ((a, w1, s1), (b, w3, s3)):
                nc.tensor.matmul_mx(
                    out=o[:],
                    lhsT=gq[:, cols].bitcast(FP8X4),
                    lhsT_scale=gs[:, cols],
                    rhs=w[:, e, :].bitcast(FP4X4),
                    rhs_scale=sc[:, f, :],
                    start=True,
                    stop=True,
                )
            sig = ring.tile([P, H], F32, name="sig")
            nc.scalar.activation(sig[:], a[:], SIGMOID)
            st["ab", e, s] = (sig, b)

        def hidden(e, s):
            if not 0 <= e < E:
                return
            if s == 0:
                turned = psum.tile([P, 2 * C], F32, name="turned")
                st["turned", e] = turned
            turned = st["turned", e]
            sig, b = st["ab", e, s]
            h = ring.tile([P, H], BF16, name="h", align_bytes=64)
            nc.vector.tensor_tensor(
                h[:].rearrange("p (u w d) -> p w u d", u=2, d=2),
                b[:].rearrange("p (w u d) -> p w u d", u=2, d=2),
                sig[:].rearrange("p (w u d) -> p w u d", u=2, d=2),
                MULT,
            )
            hw = h[:].bitcast(F32)
            for u in range(2):
                nc.tensor.transpose(
                    turned[:, C * u + 128 * s : C * u + 128 * s + 128],
                    hw[:, 128 * u : 128 * u + 128],
                    ident[:],
                )

        def turn_out(e):
            if not 0 <= e < E:
                return
            hT = ring.tile([P, 4 * C], BF16, name="hT", align_bytes=64)
            nc.scalar.copy(
                hT[:].bitcast(F32).rearrange("p (n u) -> p n u", u=2),
                st["turned", e][:].rearrange("p (u n) -> p n u", u=2),
            )
            st["h", e] = hT

        def second(e):
            if not 0 <= e < E:
                return
            hT = st["h", e]
            hq = ring.tile([P, C], U32, name="hq", align_bytes=64)
            hs = ring.tile([P, C], U8, name="hs", align_bytes=64)
            nc.vector.quantize_mx(out=hq[:].bitcast(FP8X4), scales=hs[:], in_=hT[:])
            y = psum.tile([P, 2, C], F32, name="y")
            for m in range(2):
                nc.tensor.matmul_mx(
                    out=y[:, m, :],
                    lhsT=w2[:, e, 256 * m : 256 * m + 256].bitcast(FP4X4),
                    lhsT_scale=s2[:, e, 128 * m : 128 * m + 128],
                    rhs=hq[:].bitcast(FP8X4),
                    rhs_scale=hs[:],
                    start=True,
                    stop=True,
                )
            ys = ring.tile([P, 2, C], F32, name="ys")
            nc.scalar.copy(ys[:], y[:])
            st["y", e] = ys

        def scatter(e, m):
            if not 0 <= e < E:
                return
            nc.vector.tensor_tensor(
                windows[m][:].indirect(offs_of(e)),
                st["y", e][:, m, :],
                gates[:, C * e : C * e + C],
                MULT,
            )

        gather(0)
        first(0, 0)
        first(0, 1)
        gather(1)
        for i in range(1, E + 3):
            hidden(i - 1, 0)
            first(i, 0)
            scatter(i - 3, 0)
            hidden(i - 1, 1)
            first(i, 1)
            turn_out(i - 1)
            gather(i + 1)
            if i - 3 < E - 3:
                scatter(i - 3, 1)
            elif i - 3 == E - 2:
                scatter(E - 3, 1)
            second(i - 1)
        nc.sync.dma_start(out[0:P, :], windows[0][:])
        for e in range(E - 2, E):
            scatter(e, 1)
        nc.sync.dma_start(out[P : 2 * P, :], windows[1][:])
